import numpy as np, ml_dtypes
CORES = [1,2,5,7,57,58,61,63,73,74,77,79]
N = 12
TK = 128
def setup_inputs(rng):
    return {"b": rng.standard_normal((N, 128, TK), dtype=np.float32).astype(ml_dtypes.bfloat16), "l": (rng.standard_normal((N, 128, N * 128), dtype=np.float32) / 16).astype(ml_dtypes.bfloat16)}
def setup_inputs_big(rng):
    d = setup_inputs(rng)
    for k in ("b",): d[k] = (d[k].astype(np.float32) * 1048576.0).astype(d[k].dtype)
    return d
def setup_inputs_small(rng):
    d = setup_inputs(rng)
    for k in ("b",): d[k] = (d[k].astype(np.float32) * (1 / 1048576.0)).astype(d[k].dtype)
    return d
def setup_inputs_apart(rng):
    d = setup_inputs(rng)
    f = (10.0 ** rng.permutation(np.linspace(-1.5, 1.5, N))).astype(np.float32).reshape(N, 1, 1)
    for k in ("b",): d[k] = (d[k].astype(np.float32) * f).astype(d[k].dtype)
    return d
def reference(b, l):
    B, L = b.astype(np.float64), l.astype(np.float64)
    y = np.zeros((N, 128, TK))
    for r in range(N):
        acc = B[r].copy()
        for s in range(r):
            acc -= L[r][:, 128 * s:128 * s + 128].T @ y[s]
        y[r] = acc
    return {"y": y.astype(ml_dtypes.bfloat16)}

@@ -1,0 +1,246 @@
+from concourse.bass import DstId, RemoteDMATransfer
+from concourse.mybir import dt, AluOpType
+
+W = 128
+HW = 64
+NT = 12
+
+SCRATCH = {
+    "own": ("sbuf", [128, NT * W], "bfloat16"),
+    "row0": ("sbuf", [128, NT * W], "bfloat16"),
+    "row1": ("sbuf", [128, NT * W], "bfloat16"),
+    "row2": ("sbuf", [128, NT * W], "bfloat16"),
+    "row3": ("sbuf", [128, NT * W], "bfloat16"),
+    "ya": ("sbuf", [128, 4 * W], "bfloat16"),
+    "yb": ("sbuf", [128, 4 * W], "bfloat16"),
+    "yc": ("sbuf", [128, 4 * W], "bfloat16"),
+    "yout": ("sbuf", [128, W], "bfloat16"),
+    "xch": ("sbuf", [128, W], "bfloat16"),
+}
+for _i in range(8):
+    SCRATCH["ps%d" % _i] = ("psum", [128, 512], "float32")
+
+SEMAPHORES = ["ld", "st", "snd", "r0", "r1", "r2", "r3", "sya", "syb0", "syb1", "sx"] \
+    + ["p%d" % _i for _i in range(8)] + ["d%d" % _i for _i in range(8)]
+
+ROW_ENGINES = (8, 16, 16)
+
+
+def rank_program(g, core, T, topo):
+    r = T.rank_of(core)
+    if r is None:
+        return
+    cores = T.cores
+    chips = []
+    for c in cores:
+        if topo.chip(c) not in chips:
+            chips.append(topo.chip(c))
+    grp = [[q for q in range(len(cores)) if topo.chip(cores[q]) == ch] for ch in chips]
+    gi = chips.index(topo.chip(core))
+    G = grp[gi]
+    g0 = G[0]
+    GA, GB, GC = grp
+
+    def same_die(q, lst):
+        return [x for x in lst if topo.die(cores[x]) == topo.die(cores[q])]
+
+    def pick(dst_rank, n, off=0):
+        m = topo.mask(core, cores[dst_rank])
+        bits = [e for e in range(m.bit_length()) if (m >> e) & 1][off:off + n]
+        out = 0
+        for e in bits:
+            out |= 1 << e
+        return out
+
+    sent = [0]
+
+    def xfer(src, dst, dst_ranks, sem, mask):
+        ids = []
+        for q in dst_ranks:
+            rid, pid, _se = topo.addr(cores[q])
+            ids.append(DstId(rid=rid, pnc=pid))
+        sent[0] += bin(mask).count("1")
+        return RemoteDMATransfer(dst_ids=ids, dma_engine_mask=mask, remote_sem=sem,
+                                 srcs=[src], dsts=[dst for _q in dst_ranks], alu_op=0)
+
+    solvers = [q for q in GA if all(topo.may_write(cores[q], cores[x]) for x in GB + GC)]
+    n_off = bin(topo.mask(cores[solvers[0]], cores[GB[0]])).count("1")
+
+    def b_half(q):
+        return same_die(q, GB).index(q)
+
+    def row_dests(k):
+        kg = [x for x in grp if k in x][0]
+        if kg is GA:
+            return [x for x in solvers if x != k]
+        if kg is GB:
+            return [x for x in GB if x != k]
+        return [x for x in GC if x > k]
+
+    n_row = ROW_ENGINES[gi]
+
+    wid = (r + 1) * W
+    g.sync.dma_start(T.own[:, 0:W], T.b[:, :]).then_inc(T.sem.ld, 16)
+    n_ld = 16
+    if r > 0:
+        g.scalar.dma_start(T.own[:, W:wid], T.l[:, 0:r * W]).then_inc(T.sem.ld, 16)
+        n_ld = 32
+    n_st = [0]
+
+    dests = row_dests(r)
+    g.wait_ge(T.sem.ld, n_ld)
+    if dests:
+        g.remote_dma_fused([xfer(T.own[:, 0:wid], T["row%d" % (r - g0)][:, 0:wid], dests,
+                                 T.sem["r%d" % (r - g0)], pick(dests[0], n_row))], local_sem=T.sem.snd)
+
+    def rowbuf(k):
+        return T.own if k == r else T["row%d" % (k - g0)]
+
+    def tile(k, s):
+        return rowbuf(k)[:, (s + 1) * W:(s + 2) * W]
+
+    def bvec(k, h):
+        return rowbuf(k)[:, h * HW:(h + 1) * HW]
+
+    seen = {}
+
+    def need(q, qname, sem, val):
+        if (qname, sem) not in seen:
+            seen[(qname, sem)] = 1
+            q.wait_ge(T.sem[sem], val)
+
+    def need_row(q, qname, k):
+        if k == r:
+            need(q, qname, "ld", n_ld)
+        else:
+            need(q, qname, "r%d" % (k - g0), n_row)
+
+    def slot(buf, j, h):
+        return buf[:, h * 4 * HW + j * HW: h * 4 * HW + (j + 1) * HW]
+
+    if gi == 0:
+        rows = list(GA) if r in solvers else []
+        halves = [0, 1]
+        yloc = T.ya
+    elif gi == 1:
+        rows = list(GB)
+        halves = [b_half(r)]
+        yloc = T.yb
+    else:
+        rows = [k for k in GC if k <= r]
+        halves = [0, 1]
+        yloc = T.yc
+
+    def idx(k, h):
+        return (k - g0) * 2 + h
+
+    def yout_ap(k, h):
+        if gi == 2 and k == r:
+            return T.yout[:, h * HW:(h + 1) * HW]
+        return slot(yloc, k - g0, h)
+
+    n_ya = n_off // len(same_die(r, GB)) if gi == 1 else n_off
+
+    def terms(k, h):
+        out = []
+        for s in range(k):
+            if s in GA and gi > 0:
+                out.append((tile(k, s), slot(T.ya, s - GA[0], h), "sya", n_ya))
+            elif s in GB and gi > 1:
+                out.append((tile(k, s), slot(T.yb, s - GB[0], h), "syb%d" % h, n_off))
+            elif gi == 0 and s == g0:
+                out.append((tile(k, s), bvec(s, h), None, 0))
+            else:
+                out.append((tile(k, s), slot(yloc, s - g0, h), "d%d" % idx(s, h), 1))
+        return out
+
+    pe, ve = g.tensor, g.vector
+    early = len(GA) if gi == 2 else 0
+    for k in rows:
+        for h in halves:
+            for n, (lt, rh, sem, val) in enumerate(terms(k, h)[:early]):
+                need_row(pe, "pe", k)
+                need(pe, "pe", sem, val)
+                pe.matmul(T["ps%d" % idx(k, h)][:, 0:HW], lt, rh, n == 0, False)
+    for k in rows:
+        tl = {h: terms(k, h) for h in halves}
+        nt = len(tl[halves[0]])
+        if nt == 0:
+            for h in halves:
+                need_row(ve, "ve", k)
+                ve.tensor_copy(yout_ap(k, h), bvec(k, h)).then_inc(T.sem["d%d" % idx(k, h)], 1)
+            continue
+        n_prev = min(g0, nt)
+        order = [(h, n) for h in halves for n in range(early, n_prev)] \
+            + [(h, n) for n in range(n_prev, nt) for h in halves]
+        for h, n in order:
+            lt, rh, sem, val = tl[h][n]
+            need_row(pe, "pe", k)
+            if sem is None:
+                need_row(pe, "pe", g0)
+            else:
+                need(pe, "pe", sem, val)
+            mm = pe.matmul(T["ps%d" % idx(k, h)][:, 0:HW], lt, rh, n == 0, n == nt - 1)
+            if n == nt - 1:
+                mm.then_inc(T.sem["p%d" % idx(k, h)], 1)
+        for h in halves:
+            need_row(ve, "ve", k)
+            ve.wait_ge(T.sem["p%d" % idx(k, h)], 1)
+            ve.tensor_tensor(yout_ap(k, h), bvec(k, h), T["ps%d" % idx(k, h)][:, 0:HW],
+                             AluOpType.subtract).then_inc(T.sem["d%d" % idx(k, h)], 1)
+
+    def store(q, sem, val, h, src):
+        q.wait_ge(T.sem[sem], val)
+        q.dma_start(T.y[:, h * HW:(h + 1) * HW], src).then_inc(T.sem.st, 16)
+        n_st[0] += 16
+
+    queues = [g.sync, g.scalar]
+
+    if gi == 0:
+        if r in solvers:
+            for k in rows:
+                for h in halves:
+                    g.wait_ge(T.sem["d%d" % idx(k, h)], 1)
+            mine_b = same_die(r, GB)
+            per = n_off // len(mine_b)
+            g.remote_dma_fused([xfer(T.ya[:, b_half(q) * 4 * HW:(b_half(q) + 1) * 4 * HW],
+                                     T.ya[:, b_half(q) * 4 * HW:(b_half(q) + 1) * 4 * HW],
+                                     [q], T.sem.sya, pick(q, per, j * per)) for j, q in enumerate(mine_b)],
+                               local_sem=T.sem.snd)
+            mine_c = same_die(r, GC)
+            g.remote_dma_fused([xfer(T.ya[:, :], T.ya[:, :], mine_c, T.sem.sya, pick(mine_c[0], n_off))],
+                               local_sem=T.sem.snd)
+            for q in GA:
+                if q != g0 and q not in solvers and same_die(q, solvers)[0] == r:
+                    per = n_off // 2
+                    g.remote_dma_fused([xfer(slot(T.ya, q - g0, h), T.xch[:, h * HW:(h + 1) * HW], [q], T.sem.sx,
+                                             pick(q, per, h * per)) for h in (0, 1)], local_sem=T.sem.snd)
+            for h in halves:
+                store(queues[h], "d%d" % idx(r, h), 1, h, slot(T.ya, r - g0, h))
+        elif r == g0:
+            g.scalar.wait_ge(T.sem.ld, n_ld)
+            g.scalar.dma_start(T.y[:, :], T.own[:, 0:W]).then_inc(T.sem.st, 16)
+            n_st[0] += 16
+        else:
+            g.sync.wait_ge(T.sem.sx, n_off)
+            g.sync.dma_start(T.y[:, :], T.xch[:, :]).then_inc(T.sem.st, 16)
+            n_st[0] += 16
+    elif gi == 1:
+        h = halves[0]
+        for k in rows:
+            g.wait_ge(T.sem["d%d" % idx(k, h)], 1)
+        mine_c = same_die(r, GC)
+        g.remote_dma_fused([xfer(T.yb[:, h * 4 * HW:(h + 1) * 4 * HW], T.yb[:, h * 4 * HW:(h + 1) * 4 * HW],
+                                 mine_c, T.sem["syb%d" % h], pick(mine_c[0], n_off))], local_sem=T.sem.snd)
+        partner = [q for q in same_die(r, GB) if q != r][0]
+        g.remote_dma_fused([xfer(slot(T.yb, partner - g0, h), T.xch[:, 0:HW], [partner], T.sem.sx,
+                                 pick(partner, n_off))], local_sem=T.sem.snd)
+        store(g.sync, "d%d" % idx(r, h), 1, h, slot(T.yb, r - g0, h))
+        store(g.scalar, "sx", n_off, 1 - h, T.xch[:, 0:HW])
+    else:
+        for h in halves:
+            store(queues[h], "d%d" % idx(r, h), 1, h, T.yout[:, h * HW:(h + 1) * HW])
+
+    if sent[0]:
+        g.wait_ge(T.sem.snd, sent[0])
+    g.wait_ge(T.sem.st, n_st[0])

@@ -11,16 +11,25 @@ SCRATCH = {
     "row1": ("sbuf", [128, NT * W], "bfloat16"),
     "row2": ("sbuf", [128, NT * W], "bfloat16"),
     "row3": ("sbuf", [128, NT * W], "bfloat16"),
+    "at0": ("sbuf", [128, NT * W], "bfloat16"),
+    "at1": ("sbuf", [128, NT * W], "bfloat16"),
+    "at2": ("sbuf", [128, NT * W], "bfloat16"),
     "ya": ("sbuf", [128, 4 * W], "bfloat16"),
     "yb": ("sbuf", [128, 4 * W], "bfloat16"),
-    "yc": ("sbuf", [128, 4 * W], "bfloat16"),
     "yout": ("sbuf", [128, W], "bfloat16"),
     "xch": ("sbuf", [128, W], "bfloat16"),
+    "e1": ("sbuf", [128, W + 1], "bfloat16"),
+    "zid": ("dram", [1, 128 * (W + 1)], "bfloat16"),
+    "idn": ("sbuf", [128, W], "bfloat16"),
+    "ub": ("sbuf", [128, 2 * W], "bfloat16"),
+    "mt": ("sbuf", [128, 8 * W], "bfloat16"),
 }
 for _i in range(8):
     SCRATCH["ps%d" % _i] = ("psum", [128, 512], "float32")
 
-SEMAPHORES = ["ld", "st", "snd", "r0", "r1", "r2", "r3", "sya", "syb0", "syb1", "sx"] \
+SEMAPHORES = ["ld", "st", "snd", "r0", "r1", "r2", "r3", "sya", "syb0", "syb1", "sx", "ms", "id1", "idd",
+              "up0", "up1", "uc0", "uc1", "mp0", "mp1", "mc0", "mc1"] \
+    + ["tp%d" % _i for _i in range(8)] + ["tc%d" % _i for _i in range(8)] \
     + ["p%d" % _i for _i in range(8)] + ["d%d" % _i for _i in range(8)]
 
 ROW_ENGINES = (8, 16, 16)
@@ -40,6 +49,8 @@ def rank_program(g, core, T, topo):
     G = grp[gi]
     g0 = G[0]
     GA, GB, GC = grp
+    pe, ve = g.tensor, g.vector
+    queues = [g.sync, g.scalar]
 
     def same_die(q, lst):
         return [x for x in lst if topo.die(cores[x]) == topo.die(cores[q])]
@@ -69,25 +80,30 @@ def rank_program(g, core, T, topo):
     def b_half(q):
         return same_die(q, GB).index(q)
 
-    def row_dests(k):
-        kg = [x for x in grp if k in x][0]
-        if kg is GA:
-            return [x for x in solvers if x != k]
-        if kg is GB:
-            return [x for x in GB if x != k]
-        return [x for x in GC if x > k]
-
+    if gi == 0:
+        dests = [x for x in solvers if x != r]
+    elif gi == 1:
+        dests = [x for x in GB if x != r]
+    else:
+        dests = [x for x in GC if x > r]
     n_row = ROW_ENGINES[gi]
+    lower = [k for k in GC if k < r][::-1] if gi == 2 else []
 
     wid = (r + 1) * W
     g.sync.dma_start(T.own[:, 0:W], T.b[:, :]).then_inc(T.sem.ld, 16)
     n_ld = 16
     if r > 0:
         g.scalar.dma_start(T.own[:, W:wid], T.l[:, 0:r * W]).then_inc(T.sem.ld, 16)
-        n_ld = 32
+        n_ld += 16
+    if lower:
+        ve.memset(T.e1[:, 0:1], 1.0).then_inc(T.sem.ms, 1)
+        ve.memset(T.e1[:, 1:W + 1], 0.0).then_inc(T.sem.ms, 1)
+        g.sync.wait_ge(T.sem.ms, 2)
+        g.sync.dma_start(T.zid[0], T.e1[:, :]).then_inc(T.sem.id1, 16)
+        g.sync.wait_ge(T.sem.id1, 16)
+        g.sync.dma_start(T.idn[:, :], T.zid[0, 0:128 * W]).then_inc(T.sem.idd, 16)
     n_st = [0]
 
-    dests = row_dests(r)
     g.wait_ge(T.sem.ld, n_ld)
     if dests:
         g.remote_dma_fused([xfer(T.own[:, 0:wid], T["row%d" % (r - g0)][:, 0:wid], dests,
@@ -118,60 +134,145 @@ def rank_program(g, core, T, topo):
     def slot(buf, j, h):
         return buf[:, h * 4 * HW + j * HW: h * 4 * HW + (j + 1) * HW]
 
+    def store(q, sem, val, h, src):
+        q.wait_ge(T.sem[sem], val)
+        q.dma_start(T.y[:, h * HW:(h + 1) * HW], src).then_inc(T.sem.st, 16)
+        n_st[0] += 16
+
+    if gi == 2:
+        fills = []
+        fill_of = {}
+        for k in lower:
+            for s0 in range(0, k, 4):
+                for s in range(s0, min(k, s0 + 4)):
+                    fill_of[(k, s)] = len(fills)
+                fills.append((k, s0, min(4, k - s0)))
+
+        def a_t(k, s):
+            need(pe, "pe", "tc%d" % fill_of[(k, s)], 1)
+            return T["at%d" % (k - g0)][:, s * W:(s + 1) * W]
+
+        def u_ap(k):
+            return tile(r, k) if k == r - 1 else T.ub[:, (r - 2 - k) * W:(r - 1 - k) * W]
+
+        def need_u(k):
+            if k != r - 1:
+                need(pe, "pe", "uc%d" % (r - 2 - k), 1)
+
+        need_row(pe, "pe", r)
+        need_row(ve, "ve", r)
+        for k in lower:
+            for f, (kk, s0, n) in enumerate(fills):
+                if kk != k:
+                    continue
+                bank = T["ps%d" % (2 + f % 3)]
+                need(pe, "pe", "idd", 16)
+                need_row(pe, "pe", k)
+                if f >= 3:
+                    need(pe, "pe", "tc%d" % (f - 3), 1)
+                for j in range(n):
+                    mm = pe.matmul(bank[:, j * W:(j + 1) * W], tile(k, s0 + j), T.idn[:, :], True, True)
+                mm.then_inc(T.sem["tp%d" % f], 1)
+                ve.wait_ge(T.sem["tp%d" % f], 1)
+                ve.tensor_copy(T["at%d" % (k - g0)][:, s0 * W:(s0 + n) * W],
+                               bank[:, 0:n * W]).then_inc(T.sem["tc%d" % f], 1)
+            if k - 1 >= g0:
+                kk = k - 1
+                j = r - 2 - kk
+                ms = [m for m in lower if m > kk]
+                for m in ms:
+                    lt = a_t(m, kk)
+                    need_u(m)
+                    mm = pe.matmul(T["ps%d" % (5 + j)][:, 0:W], lt, u_ap(m), m == ms[0], m == ms[-1])
+                mm.then_inc(T.sem["up%d" % j], 1)
+                ve.wait_ge(T.sem["up%d" % j], 1)
+                ve.tensor_tensor(u_ap(kk), tile(r, kk), T["ps%d" % (5 + j)][:, 0:W],
+                                 AluOpType.subtract).then_inc(T.sem["uc%d" % j], 1)
+        m_bank = (7, 5)
+        if lower:
+            for blk in (0, 1):
+                for s in range(4 * blk, 4 * blk + 4):
+                    for k in lower:
+                        lt = a_t(k, s)
+                        need_u(k)
+                        mm = pe.matmul(T["ps%d" % m_bank[blk]][:, (s % 4) * W:(s % 4 + 1) * W], lt, u_ap(k),
+                                       k == lower[0], k == lower[-1])
+                mm.then_inc(T.sem["mp%d" % blk], 1)
+                ve.wait_ge(T.sem["mp%d" % blk], 1)
+                ve.tensor_tensor(T.mt[:, blk * 512:(blk + 1) * 512], T.own[:, W + blk * 512:W + (blk + 1) * 512],
+                                 T["ps%d" % m_bank[blk]][:, 0:512], AluOpType.subtract).then_inc(T.sem["mc%d" % blk], 1)
+
+        def m_ap(s):
+            return T.mt[:, s * W:(s + 1) * W] if lower else tile(r, s)
+
+        first = {0: True, 1: True}
+
+        def acc(h, lt, rh, stop):
+            mm = pe.matmul(T["ps%d" % h][:, 0:HW], lt, rh, first[h], stop)
+            first[h] = False
+            return mm
+
+        for k in lower:
+            for h in (0, 1):
+                acc(h, u_ap(k), bvec(k, h), False)
+        if lower:
+            need(pe, "pe", "mc0", 1)
+        need(pe, "pe", "sya", n_off)
+        for h in (0, 1):
+            for s in GA:
+                acc(h, m_ap(s), slot(T.ya, s - GA[0], h), False)
+        if lower:
+            need(pe, "pe", "mc1", 1)
+        for h in (0, 1):
+            need(pe, "pe", "syb%d" % h, n_off)
+            for s in GB:
+                mm = acc(h, m_ap(s), slot(T.yb, s - GB[0], h), s == GB[-1])
+            mm.then_inc(T.sem["p%d" % h], 1)
+        for h in (0, 1):
+            ve.wait_ge(T.sem["p%d" % h], 1)
+            ve.tensor_tensor(T.yout[:, h * HW:(h + 1) * HW], bvec(r, h), T["ps%d" % h][:, 0:HW],
+                             AluOpType.subtract).then_inc(T.sem["d%d" % h], 1)
+            store(queues[h], "d%d" % h, 1, h, T.yout[:, h * HW:(h + 1) * HW])
+        if sent[0]:
+            g.wait_ge(T.sem.snd, sent[0])
+        g.wait_ge(T.sem.st, n_st[0])
+        return
+
     if gi == 0:
         rows = list(GA) if r in solvers else []
         halves = [0, 1]
         yloc = T.ya
-    elif gi == 1:
+    else:
         rows = list(GB)
         halves = [b_half(r)]
         yloc = T.yb
-    else:
-        rows = [k for k in GC if k <= r]
-        halves = [0, 1]
-        yloc = T.yc
 
     def idx(k, h):
         return (k - g0) * 2 + h
 
-    def yout_ap(k, h):
-        if gi == 2 and k == r:
-            return T.yout[:, h * HW:(h + 1) * HW]
-        return slot(yloc, k - g0, h)
-
-    n_ya = n_off // len(same_die(r, GB)) if gi == 1 else n_off
+    n_ya = n_off // len(same_die(r, GB))
 
     def terms(k, h):
         out = []
         for s in range(k):
             if s in GA and gi > 0:
                 out.append((tile(k, s), slot(T.ya, s - GA[0], h), "sya", n_ya))
-            elif s in GB and gi > 1:
-                out.append((tile(k, s), slot(T.yb, s - GB[0], h), "syb%d" % h, n_off))
             elif gi == 0 and s == g0:
                 out.append((tile(k, s), bvec(s, h), None, 0))
             else:
                 out.append((tile(k, s), slot(yloc, s - g0, h), "d%d" % idx(s, h), 1))
         return out
 
-    pe, ve = g.tensor, g.vector
-    early = len(GA) if gi == 2 else 0
-    for k in rows:
-        for h in halves:
-            for n, (lt, rh, sem, val) in enumerate(terms(k, h)[:early]):
-                need_row(pe, "pe", k)
-                need(pe, "pe", sem, val)
-                pe.matmul(T["ps%d" % idx(k, h)][:, 0:HW], lt, rh, n == 0, False)
     for k in rows:
         tl = {h: terms(k, h) for h in halves}
         nt = len(tl[halves[0]])
         if nt == 0:
             for h in halves:
                 need_row(ve, "ve", k)
-                ve.tensor_copy(yout_ap(k, h), bvec(k, h)).then_inc(T.sem["d%d" % idx(k, h)], 1)
+                ve.tensor_copy(slot(yloc, k - g0, h), bvec(k, h)).then_inc(T.sem["d%d" % idx(k, h)], 1)
             continue
         n_prev = min(g0, nt)
-        order = [(h, n) for h in halves for n in range(early, n_prev)] \
+        order = [(h, n) for h in halves for n in range(0, n_prev)] \
             + [(h, n) for n in range(n_prev, nt) for h in halves]
         for h, n in order:
             lt, rh, sem, val = tl[h][n]
@@ -186,15 +287,8 @@ def rank_program(g, core, T, topo):
         for h in halves:
             need_row(ve, "ve", k)
             ve.wait_ge(T.sem["p%d" % idx(k, h)], 1)
-            ve.tensor_tensor(yout_ap(k, h), bvec(k, h), T["ps%d" % idx(k, h)][:, 0:HW],
+            ve.tensor_tensor(slot(yloc, k - g0, h), bvec(k, h), T["ps%d" % idx(k, h)][:, 0:HW],
                              AluOpType.subtract).then_inc(T.sem["d%d" % idx(k, h)], 1)
-
-    def store(q, sem, val, h, src):
-        q.wait_ge(T.sem[sem], val)
-        q.dma_start(T.y[:, h * HW:(h + 1) * HW], src).then_inc(T.sem.st, 16)
-        n_st[0] += 16
-
-    queues = [g.sync, g.scalar]
 
     if gi == 0:
         if r in solvers:
@@ -225,7 +319,7 @@ def rank_program(g, core, T, topo):
             g.sync.wait_ge(T.sem.sx, n_off)
             g.sync.dma_start(T.y[:, :], T.xch[:, :]).then_inc(T.sem.st, 16)
             n_st[0] += 16
-    elif gi == 1:
+    else:
         h = halves[0]
         for k in rows:
             g.wait_ge(T.sem["d%d" % idx(k, h)], 1)
@@ -237,9 +331,6 @@ def rank_program(g, core, T, topo):
                                  pick(partner, n_off))], local_sem=T.sem.snd)
         store(g.sync, "d%d" % idx(r, h), 1, h, slot(T.yb, r - g0, h))
         store(g.scalar, "sx", n_off, 1 - h, T.xch[:, 0:HW])
-    else:
-        for h in halves:
-            store(queues[h], "d%d" % idx(r, h), 1, h, T.yout[:, h * HW:(h + 1) * HW])
 
     if sent[0]:
         g.wait_ge(T.sem.snd, sent[0])

@@ -7,29 +7,30 @@ NT = 12
 
 SCRATCH = {
     "own": ("sbuf", [128, NT * W], "bfloat16"),
+    "tx": ("sbuf", [128, NT * W], "bfloat16"),
     "row0": ("sbuf", [128, NT * W], "bfloat16"),
     "row1": ("sbuf", [128, NT * W], "bfloat16"),
     "row2": ("sbuf", [128, NT * W], "bfloat16"),
     "row3": ("sbuf", [128, NT * W], "bfloat16"),
-    "at0": ("sbuf", [128, NT * W], "bfloat16"),
-    "at1": ("sbuf", [128, NT * W], "bfloat16"),
-    "at2": ("sbuf", [128, NT * W], "bfloat16"),
     "ya": ("sbuf", [128, 4 * W], "bfloat16"),
     "yb": ("sbuf", [128, 4 * W], "bfloat16"),
     "yout": ("sbuf", [128, W], "bfloat16"),
     "xch": ("sbuf", [128, W], "bfloat16"),
-    "e1": ("sbuf", [128, W + 1], "bfloat16"),
-    "zid": ("dram", [1, 128 * (W + 1)], "bfloat16"),
+    "ones": ("sbuf", [128, W], "bfloat16"),
     "idn": ("sbuf", [128, W], "bfloat16"),
-    "ub": ("sbuf", [128, 2 * W], "bfloat16"),
+    "ub": ("sbuf", [128, 3 * W], "bfloat16"),
+    "bt": ("sbuf", [128, 3 * W], "bfloat16"),
+    "zb": ("sbuf", [128, 2 * HW], "bfloat16"),
     "mt": ("sbuf", [128, 8 * W], "bfloat16"),
 }
 for _i in range(8):
     SCRATCH["ps%d" % _i] = ("psum", [128, 512], "float32")
 
-SEMAPHORES = ["ld", "st", "snd", "r0", "r1", "r2", "r3", "sya", "syb0", "syb1", "sx", "ms", "id1", "idd",
-              "up0", "up1", "uc0", "uc1", "mp0", "mp1", "mc0", "mc1"] \
-    + ["tp%d" % _i for _i in range(8)] + ["tc%d" % _i for _i in range(8)] \
+SEMAPHORES = ["ld", "ldt", "st", "snd", "r0", "r1", "r2", "r3", "i0", "i1", "i2", "i3",
+              "sya", "syb0", "syb1", "sx", "ms", "idd",
+              "up0", "up1", "up2", "uc0", "uc1", "uc2", "mp0", "mp1", "mc0", "mc1",
+              "tp0", "tp1", "tp2", "tc0", "tc1", "tc2", "z0", "z1", "q0", "q1", "q2"] \
+    + ["c%d_%d" % (_i, _j) for _i in range(3) for _j in range(3)] \
     + ["p%d" % _i for _i in range(8)] + ["d%d" % _i for _i in range(8)]
 
 ROW_ENGINES = (8, 16, 16)
@@ -76,6 +77,8 @@ def rank_program(g, core, T, topo):
 
     solvers = [q for q in GA if all(topo.may_write(cores[q], cores[x]) for x in GB + GC)]
     n_off = bin(topo.mask(cores[solvers[0]], cores[GB[0]])).count("1")
+    n_on = bin(topo.mask(cores[GA[0]], cores[GA[1]])).count("1")
+    home = n_off if n_on >= 2 * n_off else 0
 
     def b_half(q):
         return same_die(q, GB).index(q)
@@ -88,6 +91,7 @@ def rank_program(g, core, T, topo):
         dests = [x for x in GC if x > r]
     n_row = ROW_ENGINES[gi]
     lower = [k for k in GC if k < r][::-1] if gi == 2 else []
+    transposes = gi == 1 or (gi == 2 and len(dests) > 0)
 
     wid = (r + 1) * W
     g.sync.dma_start(T.own[:, 0:W], T.b[:, :]).then_inc(T.sem.ld, 16)
@@ -95,18 +99,27 @@ def rank_program(g, core, T, topo):
     if r > 0:
         g.scalar.dma_start(T.own[:, W:wid], T.l[:, 0:r * W]).then_inc(T.sem.ld, 16)
         n_ld += 16
-    if lower:
-        ve.memset(T.e1[:, 0:1], 1.0).then_inc(T.sem.ms, 1)
-        ve.memset(T.e1[:, 1:W + 1], 0.0).then_inc(T.sem.ms, 1)
-        g.sync.wait_ge(T.sem.ms, 2)
-        g.sync.dma_start(T.zid[0], T.e1[:, :]).then_inc(T.sem.id1, 16)
-        g.sync.wait_ge(T.sem.id1, 16)
-        g.sync.dma_start(T.idn[:, :], T.zid[0, 0:128 * W]).then_inc(T.sem.idd, 16)
+    if gi == 2 and dests:
+        g.sync.dma_start(T.tx[:, 0:W], T.b[:, :]).then_inc(T.sem.ldt, 16)
+    if transposes:
+        ve.memset(T.ones[:, :], 1.0).then_inc(T.sem.ms, 1)
+        g.wait_ge(T.sem.ms, 1)
+        g.affine_select(T.idn[:, :], T.ones[:, :], [[-1, W]], AluOpType.is_equal, 0.0, 0, 1).then_inc(T.sem.idd, 1)
     n_st = [0]
+    myrow = T["row%d" % (r - g0)]
 
-    g.wait_ge(T.sem.ld, n_ld)
-    if dests:
-        g.remote_dma_fused([xfer(T.own[:, 0:wid], T["row%d" % (r - g0)][:, 0:wid], dests,
+    if gi == 0:
+        g.wait_ge(T.sem.ld, n_ld)
+        if dests:
+            g.remote_dma_fused([xfer(T.own[:, 0:wid], myrow[:, 0:wid], dests,
+                                     T.sem["r%d" % (r - g0)], pick(dests[0], n_row))], local_sem=T.sem.snd)
+    elif gi == 1:
+        g.wait_ge(T.sem.ld, n_ld)
+        cut = (g0 + 1) * W
+        if wid > cut:
+            g.remote_dma_fused([xfer(T.own[:, cut:wid], myrow[:, cut:wid], dests,
+                                     T.sem["i%d" % (r - g0)], pick(dests[0], n_row))], local_sem=T.sem.snd)
+        g.remote_dma_fused([xfer(T.own[:, 0:cut], myrow[:, 0:cut], dests,
                                  T.sem["r%d" % (r - g0)], pick(dests[0], n_row))], local_sem=T.sem.snd)
 
     def rowbuf(k):
@@ -139,18 +152,45 @@ def rank_program(g, core, T, topo):
         q.dma_start(T.y[:, h * HW:(h + 1) * HW], src).then_inc(T.sem.st, 16)
         n_st[0] += 16
 
+    def idx(k, h):
+        return (k - g0) * 2 + h
+
     if gi == 2:
-        fills = []
-        fill_of = {}
-        for k in lower:
-            for s0 in range(0, k, 4):
-                for s in range(s0, min(k, s0 + 4)):
-                    fill_of[(k, s)] = len(fills)
-                fills.append((k, s0, min(4, k - s0)))
+        def cid(s):
+            return 0 if s >= g0 else 1 + s // 4
+
+        need_row(pe, "pe", r)
+        need_row(ve, "ve", r)
+        if dests:
+            chunks = ([(g0, r - g0)] if r > g0 else []) + [(s0, 4) for s0 in range(0, g0, 4)]
+            for f, (s0, n) in enumerate(chunks):
+                bank = T["ps%d" % (2 + f)]
+                need(pe, "pe", "idd", 1)
+                for j in range(n):
+                    mm = pe.matmul(bank[:, j * W:(j + 1) * W], tile(r, s0 + j), T.idn[:, :], True, True)
+                mm.then_inc(T.sem["tp%d" % f], 1)
+                ve.wait_ge(T.sem["tp%d" % f], 1)
+                ve.tensor_copy(T.tx[:, (s0 + 1) * W:(s0 + n + 1) * W], bank[:, 0:n * W]).then_inc(T.sem["tc%d" % f], 1)
+            for f, (s0, n) in enumerate(chunks):
+                lo = 0 if s0 == 0 else (s0 + 1) * W
+                hi = (s0 + n + 1) * W
+                if s0 == 0:
+                    g.wait_ge(T.sem.ldt, 16)
+                g.wait_ge(T.sem["tc%d" % f], 1)
+                g.remote_dma_fused([xfer(T.tx[:, lo:hi], myrow[:, lo:hi], dests,
+                                         T.sem["c%d_%d" % (r - g0, cid(s0))], pick(dests[0], n_row))],
+                                   local_sem=T.sem.snd)
+
+        on_die = same_die(r, GC)
+        n_sya = n_off if r == on_die[0] else n_row
+        if r == on_die[0] and len(on_die) > 1:
+            g.wait_ge(T.sem.sya, n_off)
+            g.remote_dma_fused([xfer(T.ya[:, :], T.ya[:, :], on_die[1:], T.sem.sya, pick(on_die[1], n_row))],
+                               local_sem=T.sem.snd)
 
         def a_t(k, s):
-            need(pe, "pe", "tc%d" % fill_of[(k, s)], 1)
-            return T["at%d" % (k - g0)][:, s * W:(s + 1) * W]
+            need(pe, "pe", "c%d_%d" % (k - g0, cid(s)), n_row)
+            return T["row%d" % (k - g0)][:, (s + 1) * W:(s + 2) * W]
 
         def u_ap(k):
             return tile(r, k) if k == r - 1 else T.ub[:, (r - 2 - k) * W:(r - 1 - k) * W]
@@ -159,35 +199,17 @@ def rank_program(g, core, T, topo):
             if k != r - 1:
                 need(pe, "pe", "uc%d" % (r - 2 - k), 1)
 
-        need_row(pe, "pe", r)
-        need_row(ve, "ve", r)
-        for k in lower:
-            for f, (kk, s0, n) in enumerate(fills):
-                if kk != k:
-                    continue
-                bank = T["ps%d" % (2 + f % 3)]
-                need(pe, "pe", "idd", 16)
-                need_row(pe, "pe", k)
-                if f >= 3:
-                    need(pe, "pe", "tc%d" % (f - 3), 1)
-                for j in range(n):
-                    mm = pe.matmul(bank[:, j * W:(j + 1) * W], tile(k, s0 + j), T.idn[:, :], True, True)
-                mm.then_inc(T.sem["tp%d" % f], 1)
-                ve.wait_ge(T.sem["tp%d" % f], 1)
-                ve.tensor_copy(T["at%d" % (k - g0)][:, s0 * W:(s0 + n) * W],
-                               bank[:, 0:n * W]).then_inc(T.sem["tc%d" % f], 1)
-            if k - 1 >= g0:
-                kk = k - 1
-                j = r - 2 - kk
-                ms = [m for m in lower if m > kk]
-                for m in ms:
-                    lt = a_t(m, kk)
-                    need_u(m)
-                    mm = pe.matmul(T["ps%d" % (5 + j)][:, 0:W], lt, u_ap(m), m == ms[0], m == ms[-1])
-                mm.then_inc(T.sem["up%d" % j], 1)
-                ve.wait_ge(T.sem["up%d" % j], 1)
-                ve.tensor_tensor(u_ap(kk), tile(r, kk), T["ps%d" % (5 + j)][:, 0:W],
-                                 AluOpType.subtract).then_inc(T.sem["uc%d" % j], 1)
+        for kk in lower[1:]:
+            j = r - 2 - kk
+            ms = [m for m in lower if m > kk]
+            for m in ms:
+                lt = a_t(m, kk)
+                need_u(m)
+                mm = pe.matmul(T["ps%d" % (5 + j)][:, 0:W], lt, u_ap(m), m == ms[0], m == ms[-1])
+            mm.then_inc(T.sem["up%d" % j], 1)
+            ve.wait_ge(T.sem["up%d" % j], 1)
+            ve.tensor_tensor(u_ap(kk), tile(r, kk), T["ps%d" % (5 + j)][:, 0:W],
+                             AluOpType.subtract).then_inc(T.sem["uc%d" % j], 1)
         m_bank = (7, 5)
         if lower:
             for blk in (0, 1):
@@ -213,11 +235,13 @@ def rank_program(g, core, T, topo):
             return mm
 
         for k in lower:
+            need(pe, "pe", "c%d_%d" % (k - g0, cid(0)), n_row)
+            need_u(k)
             for h in (0, 1):
                 acc(h, u_ap(k), bvec(k, h), False)
         if lower:
             need(pe, "pe", "mc0", 1)
-        need(pe, "pe", "sya", n_off)
+        need(pe, "pe", "sya", n_sya)
         for h in (0, 1):
             for s in GA:
                 acc(h, m_ap(s), slot(T.ya, s - GA[0], h), False)
@@ -238,29 +262,131 @@ def rank_program(g, core, T, topo):
         g.wait_ge(T.sem.st, n_st[0])
         return
 
-    if gi == 0:
-        rows = list(GA) if r in solvers else []
-        halves = [0, 1]
-        yloc = T.ya
-    else:
-        rows = list(GB)
-        halves = [b_half(r)]
-        yloc = T.yb
+    if gi == 1:
+        h = b_half(r)
+        n_ya = n_off // len(same_die(r, GB))
+        free = [j * 2 + (1 - h) for j in range(4)]
+        top = GB[-1]
 
-    def idx(k, h):
-        return (k - g0) * 2 + h
+        def need_tile(q, qname, k, s):
+            if k == r:
+                need(q, qname, "ld", n_ld)
+            elif s >= g0:
+                need(q, qname, "i%d" % (k - g0), n_row)
+            else:
+                need(q, qname, "r%d" % (k - g0), n_row)
 
-    n_ya = n_off // len(same_die(r, GB))
+        tpairs = [(m, k) for m in GB[:-1] for k in GB if k < m]
+        tbank = T["ps%d" % free[0]]
+        need(pe, "pe", "idd", 1)
+        for t, (m, k) in enumerate(tpairs):
+            need_tile(pe, "pe", m, k)
+            mm = pe.matmul(tbank[:, t * W:(t + 1) * W], tile(m, k), T.idn[:, :], True, True)
+        mm.then_inc(T.sem.tp0, 1)
+        ve.wait_ge(T.sem.tp0, 1)
+        ve.tensor_copy(T.bt[:, 0:len(tpairs) * W], tbank[:, 0:len(tpairs) * W]).then_inc(T.sem.tc0, 1)
+
+        def b_t(m, k):
+            t = tpairs.index((m, k))
+            return T.bt[:, t * W:(t + 1) * W]
+
+        comp = [(kr, k) for kr in GB for k in [m for m in GB if m < kr - 1][::-1]]
+
+        def u_of(kr, k):
+            if k == kr - 1:
+                return tile(kr, k)
+            i = comp.index((kr, k))
+            return T.ub[:, i * W:(i + 1) * W]
+
+        def need_uf(kr, k):
+            if k == kr - 1:
+                need_tile(pe, "pe", kr, k)
+            else:
+                need(pe, "pe", "uc%d" % comp.index((kr, k)), 1)
+
+        need(pe, "pe", "tc0", 1)
+        for i, (kr, k) in enumerate(comp):
+            bank = T["ps%d" % free[1 + i]]
+            ms = [m for m in GB if k < m < kr][::-1]
+            for m in ms:
+                need_uf(kr, m)
+                mm = pe.matmul(bank[:, 0:W], b_t(m, k), u_of(kr, m), m == ms[0], m == ms[-1])
+            mm.then_inc(T.sem["up%d" % i], 1)
+            ve.wait_ge(T.sem["up%d" % i], 1)
+            need_tile(ve, "ve", kr, k)
+            ve.tensor_tensor(u_of(kr, k), tile(kr, k), bank[:, 0:W], AluOpType.subtract).then_inc(T.sem["uc%d" % i], 1)
+
+        def z_ap(m):
+            return slot(T.yb, 0, h) if m == g0 else T.zb[:, (m - g0 - 1) * HW:(m - g0) * HW]
+
+        def z_sem(m):
+            return "d%d" % idx(g0, h) if m == g0 else "z%d" % (m - g0 - 1)
+
+        for k in GB:
+            need_tile(pe, "pe", k, GA[0])
+        need(pe, "pe", "sya", n_ya)
+        for k in GB:
+            for s in GA:
+                mm = pe.matmul(T["ps%d" % idx(k, h)][:, 0:HW], tile(k, s), slot(T.ya, s - GA[0], h),
+                               s == GA[0], s == GA[-1] and k != top)
+            if k != top:
+                mm.then_inc(T.sem["p%d" % idx(k, h)], 1)
+        for k in GB[:-1]:
+            need_tile(ve, "ve", k, GA[0])
+            ve.wait_ge(T.sem["p%d" % idx(k, h)], 1)
+            ve.tensor_tensor(z_ap(k), bvec(k, h), T["ps%d" % idx(k, h)][:, 0:HW],
+                             AluOpType.subtract).then_inc(T.sem[z_sem(k)], 1)
+
+        def bank2(k):
+            return T["ps%d" % idx(k, h)] if k == top else T["ps%d" % free[k - g0 - 1]]
+
+        for i in range(len(comp)):
+            need(pe, "pe", "uc%d" % i, 1)
+        for m in GB[:-1]:
+            need(pe, "pe", z_sem(m), 1)
+            for k in GB:
+                if k <= m:
+                    continue
+                need_uf(k, m)
+                mm = pe.matmul(bank2(k)[:, 0:HW], u_of(k, m), z_ap(m), m == g0 and k != top, m == k - 1)
+                if m == k - 1:
+                    mm.then_inc(T.sem["q%d" % (k - g0 - 1)], 1)
+        for k in GB[1:]:
+            ve.wait_ge(T.sem["q%d" % (k - g0 - 1)], 1)
+            if k == top:
+                need_tile(ve, "ve", k, GA[0])
+                src = bvec(k, h)
+            else:
+                need(ve, "ve", z_sem(k), 1)
+                src = z_ap(k)
+            ve.tensor_tensor(slot(T.yb, k - g0, h), src, bank2(k)[:, 0:HW],
+                             AluOpType.subtract).then_inc(T.sem["d%d" % idx(k, h)], 1)
+
+        for k in GB:
+            g.wait_ge(T.sem["d%d" % idx(k, h)], 1)
+        mine_c = same_die(r, GC)
+        g.remote_dma_fused([xfer(T.yb[:, h * 4 * HW:(h + 1) * 4 * HW], T.yb[:, h * 4 * HW:(h + 1) * 4 * HW],
+                                 mine_c, T.sem["syb%d" % h], pick(mine_c[0], n_off))], local_sem=T.sem.snd)
+        partner = [q for q in same_die(r, GB) if q != r][0]
+        g.remote_dma_fused([xfer(slot(T.yb, partner - g0, h), T.xch[:, 0:HW], [partner], T.sem.sx,
+                                 pick(partner, n_off, home))], local_sem=T.sem.snd)
+        store(g.sync, "d%d" % idx(r, h), 1, h, slot(T.yb, r - g0, h))
+        store(g.scalar, "sx", n_off, 1 - h, T.xch[:, 0:HW])
+        g.wait_ge(T.sem.snd, sent[0])
+        g.wait_ge(T.sem.st, n_st[0])
+        return
+
+    rows = list(GA) if r in solvers else []
+    halves = [0, 1]
+    yloc = T.ya
 
     def terms(k, h):
         out = []
         for s in range(k):
-            if s in GA and gi > 0:
-                out.append((tile(k, s), slot(T.ya, s - GA[0], h), "sya", n_ya))
-            elif gi == 0 and s == g0:
-                out.append((tile(k, s), bvec(s, h), None, 0))
+            if s == g0:
+                out.append((tile(k, s), bvec(s, h), None))
             else:
-                out.append((tile(k, s), slot(yloc, s - g0, h), "d%d" % idx(s, h), 1))
+                out.append((tile(k, s), slot(yloc, s - g0, h), "d%d" % idx(s, h)))
         return out
 
     for k in rows:
@@ -271,16 +397,13 @@ def rank_program(g, core, T, topo):
                 need_row(ve, "ve", k)
                 ve.tensor_copy(slot(yloc, k - g0, h), bvec(k, h)).then_inc(T.sem["d%d" % idx(k, h)], 1)
             continue
-        n_prev = min(g0, nt)
-        order = [(h, n) for h in halves for n in range(0, n_prev)] \
-            + [(h, n) for n in range(n_prev, nt) for h in halves]
-        for h, n in order:
-            lt, rh, sem, val = tl[h][n]
+        for h, n in [(h, n) for n in range(nt) for h in halves]:
+            lt, rh, sem = tl[h][n]
             need_row(pe, "pe", k)
             if sem is None:
                 need_row(pe, "pe", g0)
             else:
-                need(pe, "pe", sem, val)
+                need(pe, "pe", sem, 1)
             mm = pe.matmul(T["ps%d" % idx(k, h)][:, 0:HW], lt, rh, n == 0, n == nt - 1)
             if n == nt - 1:
                 mm.then_inc(T.sem["p%d" % idx(k, h)], 1)
@@ -290,47 +413,34 @@ def rank_program(g, core, T, topo):
             ve.tensor_tensor(slot(yloc, k - g0, h), bvec(k, h), T["ps%d" % idx(k, h)][:, 0:HW],
                              AluOpType.subtract).then_inc(T.sem["d%d" % idx(k, h)], 1)
 
-    if gi == 0:
-        if r in solvers:
-            for k in rows:
-                for h in halves:
-                    g.wait_ge(T.sem["d%d" % idx(k, h)], 1)
-            mine_b = same_die(r, GB)
-            per = n_off // len(mine_b)
-            g.remote_dma_fused([xfer(T.ya[:, b_half(q) * 4 * HW:(b_half(q) + 1) * 4 * HW],
-                                     T.ya[:, b_half(q) * 4 * HW:(b_half(q) + 1) * 4 * HW],
-                                     [q], T.sem.sya, pick(q, per, j * per)) for j, q in enumerate(mine_b)],
-                               local_sem=T.sem.snd)
-            mine_c = same_die(r, GC)
-            g.remote_dma_fused([xfer(T.ya[:, :], T.ya[:, :], mine_c, T.sem.sya, pick(mine_c[0], n_off))],
-                               local_sem=T.sem.snd)
-            for q in GA:
-                if q != g0 and q not in solvers and same_die(q, solvers)[0] == r:
-                    per = n_off // 2
-                    g.remote_dma_fused([xfer(slot(T.ya, q - g0, h), T.xch[:, h * HW:(h + 1) * HW], [q], T.sem.sx,
-                                             pick(q, per, h * per)) for h in (0, 1)], local_sem=T.sem.snd)
-            for h in halves:
-                store(queues[h], "d%d" % idx(r, h), 1, h, slot(T.ya, r - g0, h))
-        elif r == g0:
-            g.scalar.wait_ge(T.sem.ld, n_ld)
-            g.scalar.dma_start(T.y[:, :], T.own[:, 0:W]).then_inc(T.sem.st, 16)
-            n_st[0] += 16
-        else:
-            g.sync.wait_ge(T.sem.sx, n_off)
-            g.sync.dma_start(T.y[:, :], T.xch[:, :]).then_inc(T.sem.st, 16)
-            n_st[0] += 16
-    else:
-        h = halves[0]
+    if r in solvers:
         for k in rows:
-            g.wait_ge(T.sem["d%d" % idx(k, h)], 1)
-        mine_c = same_die(r, GC)
-        g.remote_dma_fused([xfer(T.yb[:, h * 4 * HW:(h + 1) * 4 * HW], T.yb[:, h * 4 * HW:(h + 1) * 4 * HW],
-                                 mine_c, T.sem["syb%d" % h], pick(mine_c[0], n_off))], local_sem=T.sem.snd)
-        partner = [q for q in same_die(r, GB) if q != r][0]
-        g.remote_dma_fused([xfer(slot(T.yb, partner - g0, h), T.xch[:, 0:HW], [partner], T.sem.sx,
-                                 pick(partner, n_off))], local_sem=T.sem.snd)
-        store(g.sync, "d%d" % idx(r, h), 1, h, slot(T.yb, r - g0, h))
-        store(g.scalar, "sx", n_off, 1 - h, T.xch[:, 0:HW])
+            for h in halves:
+                g.wait_ge(T.sem["d%d" % idx(k, h)], 1)
+        mine_b = same_die(r, GB)
+        per = n_off // len(mine_b)
+        g.remote_dma_fused([xfer(T.ya[:, b_half(q) * 4 * HW:(b_half(q) + 1) * 4 * HW],
+                                 T.ya[:, b_half(q) * 4 * HW:(b_half(q) + 1) * 4 * HW],
+                                 [q], T.sem.sya, pick(q, per, j * per)) for j, q in enumerate(mine_b)],
+                           local_sem=T.sem.snd)
+        first_c = same_die(r, GC)[0]
+        g.remote_dma_fused([xfer(T.ya[:, :], T.ya[:, :], [first_c], T.sem.sya, pick(first_c, n_off))],
+                           local_sem=T.sem.snd)
+        for q in GA:
+            if q != g0 and q not in solvers and same_die(q, solvers)[0] == r:
+                per = n_off // 2
+                g.remote_dma_fused([xfer(slot(T.ya, q - g0, h), T.xch[:, h * HW:(h + 1) * HW], [q], T.sem.sx,
+                                         pick(q, per, home + h * per)) for h in (0, 1)], local_sem=T.sem.snd)
+        for h in halves:
+            store(queues[h], "d%d" % idx(r, h), 1, h, slot(T.ya, r - g0, h))
+    elif r == g0:
+        g.scalar.wait_ge(T.sem.ld, n_ld)
+        g.scalar.dma_start(T.y[:, :], T.own[:, 0:W]).then_inc(T.sem.st, 16)
+        n_st[0] += 16
+    else:
+        g.sync.wait_ge(T.sem.sx, n_off)
+        g.sync.dma_start(T.y[:, :], T.xch[:, :]).then_inc(T.sem.st, 16)
+        n_st[0] += 16
 
     if sent[0]:
         g.wait_ge(T.sem.snd, sent[0])

@@ -4,6 +4,7 @@ from concourse.mybir import dt, AluOpType
 W = 128
 HW = 64
 NT = 12
+EARLY = 2
 
 SCRATCH = {
     "own": ("sbuf", [128, NT * W], "bfloat16"),
@@ -26,8 +27,8 @@ SCRATCH = {
 for _i in range(8):
     SCRATCH["ps%d" % _i] = ("psum", [128, 512], "float32")
 
-SEMAPHORES = ["ld", "ldt", "st", "snd", "r0", "r1", "r2", "r3", "i0", "i1", "i2", "i3",
-              "sya", "syb0", "syb1", "sx", "ms", "idd",
+SEMAPHORES = ["ld", "l0", "l1", "l2", "st", "snd", "r0", "r1", "r2", "r3", "i0", "i1", "i2", "i3",
+              "sya", "sya2", "sye0", "sye1", "syb0", "syb1", "sx", "ms", "idd", "cb0", "cb1", "cb2",
               "up0", "up1", "up2", "uc0", "uc1", "uc2", "mp0", "mp1", "mc0", "mc1",
               "tp0", "tp1", "tp2", "tc0", "tc1", "tc2", "z0", "z1", "q0", "q1", "q2"] \
     + ["c%d_%d" % (_i, _j) for _i in range(3) for _j in range(3)] \
@@ -83,6 +84,9 @@ def rank_program(g, core, T, topo):
     def b_half(q):
         return same_die(q, GB).index(q)
 
+    def cid(s):
+        return 0 if s >= GC[0] else 1 + s // 4
+
     if gi == 0:
         dests = [x for x in solvers if x != r]
     elif gi == 1:
@@ -94,13 +98,19 @@ def rank_program(g, core, T, topo):
     transposes = gi == 1 or (gi == 2 and len(dests) > 0)
 
     wid = (r + 1) * W
-    g.sync.dma_start(T.own[:, 0:W], T.b[:, :]).then_inc(T.sem.ld, 16)
     n_ld = 16
-    if r > 0:
-        g.scalar.dma_start(T.own[:, W:wid], T.l[:, 0:r * W]).then_inc(T.sem.ld, 16)
-        n_ld += 16
-    if gi == 2 and dests:
-        g.sync.dma_start(T.tx[:, 0:W], T.b[:, :]).then_inc(T.sem.ldt, 16)
+    chunks = []
+    if gi == 2:
+        chunks = ([(g0, r - g0)] if r > g0 else []) + [(s0, 4) for s0 in range(0, g0, 4)]
+        for f, (s0, n) in enumerate(chunks):
+            queues[(f + 1) % 2].dma_start(T.own[:, (s0 + 1) * W:(s0 + n + 1) * W],
+                                          T.l[:, s0 * W:(s0 + n) * W]).then_inc(T.sem["l%d" % cid(s0)], 16)
+        queues[(len(chunks) + 1) % 2].dma_start(T.own[:, 0:W], T.b[:, :]).then_inc(T.sem.ld, 16)
+    else:
+        g.sync.dma_start(T.own[:, 0:W], T.b[:, :]).then_inc(T.sem.ld, 16)
+        if r > 0:
+            g.scalar.dma_start(T.own[:, W:wid], T.l[:, 0:r * W]).then_inc(T.sem.ld, 16)
+            n_ld += 16
     if transposes:
         ve.memset(T.ones[:, :], 1.0).then_inc(T.sem.ms, 1)
         g.wait_ge(T.sem.ms, 1)
@@ -156,30 +166,29 @@ def rank_program(g, core, T, topo):
         return (k - g0) * 2 + h
 
     if gi == 2:
-        def cid(s):
-            return 0 if s >= g0 else 1 + s // 4
+        def need_own(q, qname, s):
+            need(q, qname, "l%d" % cid(s), 16)
 
-        need_row(pe, "pe", r)
-        need_row(ve, "ve", r)
         if dests:
-            chunks = ([(g0, r - g0)] if r > g0 else []) + [(s0, 4) for s0 in range(0, g0, 4)]
             for f, (s0, n) in enumerate(chunks):
                 bank = T["ps%d" % (2 + f)]
                 need(pe, "pe", "idd", 1)
+                need_own(pe, "pe", s0)
                 for j in range(n):
                     mm = pe.matmul(bank[:, j * W:(j + 1) * W], tile(r, s0 + j), T.idn[:, :], True, True)
                 mm.then_inc(T.sem["tp%d" % f], 1)
                 ve.wait_ge(T.sem["tp%d" % f], 1)
                 ve.tensor_copy(T.tx[:, (s0 + 1) * W:(s0 + n + 1) * W], bank[:, 0:n * W]).then_inc(T.sem["tc%d" % f], 1)
             for f, (s0, n) in enumerate(chunks):
-                lo = 0 if s0 == 0 else (s0 + 1) * W
+                lo = (s0 + 1) * W
                 hi = (s0 + n + 1) * W
-                if s0 == 0:
-                    g.wait_ge(T.sem.ldt, 16)
                 g.wait_ge(T.sem["tc%d" % f], 1)
                 g.remote_dma_fused([xfer(T.tx[:, lo:hi], myrow[:, lo:hi], dests,
                                          T.sem["c%d_%d" % (r - g0, cid(s0))], pick(dests[0], n_row))],
                                    local_sem=T.sem.snd)
+            g.wait_ge(T.sem.ld, n_ld)
+            g.remote_dma_fused([xfer(T.own[:, 0:W], myrow[:, 0:W], dests,
+                                     T.sem["cb%d" % (r - g0)], pick(dests[0], n_row))], local_sem=T.sem.snd)
 
         on_die = same_die(r, GC)
         n_sya = n_off if r == on_die[0] else n_row
@@ -196,7 +205,9 @@ def rank_program(g, core, T, topo):
             return tile(r, k) if k == r - 1 else T.ub[:, (r - 2 - k) * W:(r - 1 - k) * W]
 
         def need_u(k):
-            if k != r - 1:
+            if k == r - 1:
+                need_own(pe, "pe", k)
+            else:
                 need(pe, "pe", "uc%d" % (r - 2 - k), 1)
 
         for kk in lower[1:]:
@@ -208,6 +219,7 @@ def rank_program(g, core, T, topo):
                 mm = pe.matmul(T["ps%d" % (5 + j)][:, 0:W], lt, u_ap(m), m == ms[0], m == ms[-1])
             mm.then_inc(T.sem["up%d" % j], 1)
             ve.wait_ge(T.sem["up%d" % j], 1)
+            need_own(ve, "ve", kk)
             ve.tensor_tensor(u_ap(kk), tile(r, kk), T["ps%d" % (5 + j)][:, 0:W],
                              AluOpType.subtract).then_inc(T.sem["uc%d" % j], 1)
         m_bank = (7, 5)
@@ -221,11 +233,15 @@ def rank_program(g, core, T, topo):
                                        k == lower[0], k == lower[-1])
                 mm.then_inc(T.sem["mp%d" % blk], 1)
                 ve.wait_ge(T.sem["mp%d" % blk], 1)
+                need_own(ve, "ve", 4 * blk)
                 ve.tensor_tensor(T.mt[:, blk * 512:(blk + 1) * 512], T.own[:, W + blk * 512:W + (blk + 1) * 512],
                                  T["ps%d" % m_bank[blk]][:, 0:512], AluOpType.subtract).then_inc(T.sem["mc%d" % blk], 1)
 
         def m_ap(s):
-            return T.mt[:, s * W:(s + 1) * W] if lower else tile(r, s)
+            if lower:
+                return T.mt[:, s * W:(s + 1) * W]
+            need_own(pe, "pe", s)
+            return tile(r, s)
 
         first = {0: True, 1: True}
 
@@ -235,7 +251,7 @@ def rank_program(g, core, T, topo):
             return mm
 
         for k in lower:
-            need(pe, "pe", "c%d_%d" % (k - g0, cid(0)), n_row)
+            need(pe, "pe", "cb%d" % (k - g0), n_row)
             need_u(k)
             for h in (0, 1):
                 acc(h, u_ap(k), bvec(k, h), False)
@@ -248,10 +264,14 @@ def rank_program(g, core, T, topo):
         if lower:
             need(pe, "pe", "mc1", 1)
         for h in (0, 1):
+            need(pe, "pe", "sye%d" % h, n_off)
+            acc(h, m_ap(GB[0]), slot(T.yb, 0, h), False)
+        for h in (0, 1):
             need(pe, "pe", "syb%d" % h, n_off)
-            for s in GB:
+            for s in GB[1:]:
                 mm = acc(h, m_ap(s), slot(T.yb, s - GB[0], h), s == GB[-1])
             mm.then_inc(T.sem["p%d" % h], 1)
+        need(ve, "ve", "ld", n_ld)
         for h in (0, 1):
             ve.wait_ge(T.sem["p%d" % h], 1)
             ve.tensor_tensor(T.yout[:, h * HW:(h + 1) * HW], bvec(r, h), T["ps%d" % h][:, 0:HW],
@@ -326,9 +346,13 @@ def rank_program(g, core, T, topo):
             need_tile(pe, "pe", k, GA[0])
         need(pe, "pe", "sya", n_ya)
         for k in GB:
-            for s in GA:
+            for s in GA[:EARLY]:
+                pe.matmul(T["ps%d" % idx(k, h)][:, 0:HW], tile(k, s), slot(T.ya, s - GA[0], h), s == GA[0], False)
+        need(pe, "pe", "sya2", n_ya)
+        for k in GB:
+            for s in GA[EARLY:]:
                 mm = pe.matmul(T["ps%d" % idx(k, h)][:, 0:HW], tile(k, s), slot(T.ya, s - GA[0], h),
-                               s == GA[0], s == GA[-1] and k != top)
+                               False, s == GA[-1] and k != top)
             if k != top:
                 mm.then_inc(T.sem["p%d" % idx(k, h)], 1)
         for k in GB[:-1]:
@@ -362,10 +386,13 @@ def rank_program(g, core, T, topo):
             ve.tensor_tensor(slot(T.yb, k - g0, h), src, bank2(k)[:, 0:HW],
                              AluOpType.subtract).then_inc(T.sem["d%d" % idx(k, h)], 1)
 
-        for k in GB:
-            g.wait_ge(T.sem["d%d" % idx(k, h)], 1)
         mine_c = same_die(r, GC)
-        g.remote_dma_fused([xfer(T.yb[:, h * 4 * HW:(h + 1) * 4 * HW], T.yb[:, h * 4 * HW:(h + 1) * 4 * HW],
+        g.wait_ge(T.sem["d%d" % idx(g0, h)], 1)
+        g.remote_dma_fused([xfer(slot(T.yb, 0, h), slot(T.yb, 0, h), mine_c, T.sem["sye%d" % h],
+                                 pick(mine_c[0], n_off))], local_sem=T.sem.snd)
+        for k in GB[1:]:
+            g.wait_ge(T.sem["d%d" % idx(k, h)], 1)
+        g.remote_dma_fused([xfer(T.yb[:, h * 4 * HW + HW:(h + 1) * 4 * HW], T.yb[:, h * 4 * HW + HW:(h + 1) * 4 * HW],
                                  mine_c, T.sem["syb%d" % h], pick(mine_c[0], n_off))], local_sem=T.sem.snd)
         partner = [q for q in same_die(r, GB) if q != r][0]
         g.remote_dma_fused([xfer(slot(T.yb, partner - g0, h), T.xch[:, 0:HW], [partner], T.sem.sx,
@@ -414,15 +441,19 @@ def rank_program(g, core, T, topo):
                              AluOpType.subtract).then_inc(T.sem["d%d" % idx(k, h)], 1)
 
     if r in solvers:
-        for k in rows:
-            for h in halves:
-                g.wait_ge(T.sem["d%d" % idx(k, h)], 1)
         mine_b = same_die(r, GB)
         per = n_off // len(mine_b)
-        g.remote_dma_fused([xfer(T.ya[:, b_half(q) * 4 * HW:(b_half(q) + 1) * 4 * HW],
-                                 T.ya[:, b_half(q) * 4 * HW:(b_half(q) + 1) * 4 * HW],
-                                 [q], T.sem.sya, pick(q, per, j * per)) for j, q in enumerate(mine_b)],
-                           local_sem=T.sem.snd)
+
+        def piece(hh, j0, j1):
+            return T.ya[:, hh * 4 * HW + j0 * HW: hh * 4 * HW + j1 * HW]
+
+        for (j0, j1, sem) in ((0, EARLY, T.sem.sya), (EARLY, len(rows), T.sem.sya2)):
+            for k in rows[j0:j1]:
+                for h in halves:
+                    g.wait_ge(T.sem["d%d" % idx(k, h)], 1)
+            g.remote_dma_fused([xfer(piece(b_half(q), j0, j1), piece(b_half(q), j0, j1),
+                                     [q], sem, pick(q, per, j * per)) for j, q in enumerate(mine_b)],
+                               local_sem=T.sem.snd)
         first_c = same_die(r, GC)[0]
         g.remote_dma_fused([xfer(T.ya[:, :], T.ya[:, :], [first_c], T.sem.sya, pick(first_c, n_off))],
                            local_sem=T.sem.snd)

from concourse.bass import DstId, RemoteDMATransfer
from concourse.mybir import dt, AluOpType

W = 128
HW = 64
NT = 12
EARLY = 2

SCRATCH = {
    "own": ("sbuf", [128, NT * W], "bfloat16"),
    "tx": ("sbuf", [128, NT * W], "bfloat16"),
    "row0": ("sbuf", [128, NT * W], "bfloat16"),
    "row1": ("sbuf", [128, NT * W], "bfloat16"),
    "row2": ("sbuf", [128, NT * W], "bfloat16"),
    "row3": ("sbuf", [128, NT * W], "bfloat16"),
    "ya": ("sbuf", [128, 4 * W], "bfloat16"),
    "yb": ("sbuf", [128, 4 * W], "bfloat16"),
    "yout": ("sbuf", [128, W], "bfloat16"),
    "xch": ("sbuf", [128, W], "bfloat16"),
    "ones": ("sbuf", [128, W], "bfloat16"),
    "idn": ("sbuf", [128, W], "bfloat16"),
    "ub": ("sbuf", [128, 3 * W], "bfloat16"),
    "bt": ("sbuf", [128, 3 * W], "bfloat16"),
    "zb": ("sbuf", [128, 2 * HW], "bfloat16"),
    "mt": ("sbuf", [128, 8 * W], "bfloat16"),
}
for _i in range(8):
    SCRATCH["ps%d" % _i] = ("psum", [128, 512], "float32")

SEMAPHORES = ["ld", "l0", "l1", "l2", "st", "snd", "r0", "r1", "r2", "r3", "i0", "i1", "i2", "i3",
              "sya", "sya2", "sye0", "sye1", "syb0", "syb1", "sx", "ms", "idd", "cb0", "cb1", "cb2",
              "up0", "up1", "up2", "uc0", "uc1", "uc2", "mp0", "mp1", "mc0", "mc1",
              "tp0", "tp1", "tp2", "tc0", "tc1", "tc2", "z0", "z1", "q0", "q1", "q2"] \
    + ["c%d_%d" % (_i, _j) for _i in range(3) for _j in range(3)] \
    + ["p%d" % _i for _i in range(8)] + ["d%d" % _i for _i in range(8)]

ROW_ENGINES = (8, 16, 16)


def rank_program(g, core, T, topo):
    r = T.rank_of(core)
    if r is None:
        return
    cores = T.cores
    chips = []
    for c in cores:
        if topo.chip(c) not in chips:
            chips.append(topo.chip(c))
    grp = [[q for q in range(len(cores)) if topo.chip(cores[q]) == ch] for ch in chips]
    gi = chips.index(topo.chip(core))
    G = grp[gi]
    g0 = G[0]
    GA, GB, GC = grp
    pe, ve = g.tensor, g.vector
    queues = [g.sync, g.scalar]

    def same_die(q, lst):
        return [x for x in lst if topo.die(cores[x]) == topo.die(cores[q])]

    def pick(dst_rank, n, off=0):
        m = topo.mask(core, cores[dst_rank])
        bits = [e for e in range(m.bit_length()) if (m >> e) & 1][off:off + n]
        out = 0
        for e in bits:
            out |= 1 << e
        return out

    sent = [0]

    def xfer(src, dst, dst_ranks, sem, mask):
        ids = []
        for q in dst_ranks:
            rid, pid, _se = topo.addr(cores[q])
            ids.append(DstId(rid=rid, pnc=pid))
        sent[0] += bin(mask).count("1")
        return RemoteDMATransfer(dst_ids=ids, dma_engine_mask=mask, remote_sem=sem,
                                 srcs=[src], dsts=[dst for _q in dst_ranks], alu_op=0)

    solvers = [q for q in GA if all(topo.may_write(cores[q], cores[x]) for x in GB + GC)]
    n_off = bin(topo.mask(cores[solvers[0]], cores[GB[0]])).count("1")
    n_on = bin(topo.mask(cores[GA[0]], cores[GA[1]])).count("1")
    home = n_off if n_on >= 2 * n_off else 0

    def b_half(q):
        return same_die(q, GB).index(q)

    def cid(s):
        return 0 if s >= GC[0] else 1 + s // 4

    if gi == 0:
        dests = [x for x in solvers if x != r]
    elif gi == 1:
        dests = [x for x in GB if x != r]
    else:
        dests = [x for x in GC if x > r]
    n_row = ROW_ENGINES[gi]
    lower = [k for k in GC if k < r][::-1] if gi == 2 else []
    transposes = gi == 1 or (gi == 2 and len(dests) > 0)

    wid = (r + 1) * W
    n_ld = 16
    chunks = []
    if gi == 2:
        chunks = ([(g0, r - g0)] if r > g0 else []) + [(s0, 4) for s0 in range(0, g0, 4)]
        for f, (s0, n) in enumerate(chunks):
            queues[(f + 1) % 2].dma_start(T.own[:, (s0 + 1) * W:(s0 + n + 1) * W],
                                          T.l[:, s0 * W:(s0 + n) * W]).then_inc(T.sem["l%d" % cid(s0)], 16)
        queues[(len(chunks) + 1) % 2].dma_start(T.own[:, 0:W], T.b[:, :]).then_inc(T.sem.ld, 16)
    else:
        g.sync.dma_start(T.own[:, 0:W], T.b[:, :]).then_inc(T.sem.ld, 16)
        if r > 0:
            g.scalar.dma_start(T.own[:, W:wid], T.l[:, 0:r * W]).then_inc(T.sem.ld, 16)
            n_ld += 16
    if transposes:
        ve.memset(T.ones[:, :], 1.0).then_inc(T.sem.ms, 1)
        g.wait_ge(T.sem.ms, 1)
        g.affine_select(T.idn[:, :], T.ones[:, :], [[-1, W]], AluOpType.is_equal, 0.0, 0, 1).then_inc(T.sem.idd, 1)
    n_st = [0]
    myrow = T["row%d" % (r - g0)]

    if gi == 0:
        g.wait_ge(T.sem.ld, n_ld)
        if dests:
            g.remote_dma_fused([xfer(T.own[:, 0:wid], myrow[:, 0:wid], dests,
                                     T.sem["r%d" % (r - g0)], pick(dests[0], n_row))], local_sem=T.sem.snd)
    elif gi == 1:
        g.wait_ge(T.sem.ld, n_ld)
        cut = (g0 + 1) * W
        if wid > cut:
            g.remote_dma_fused([xfer(T.own[:, cut:wid], myrow[:, cut:wid], dests,
                                     T.sem["i%d" % (r - g0)], pick(dests[0], n_row))], local_sem=T.sem.snd)
        g.remote_dma_fused([xfer(T.own[:, 0:cut], myrow[:, 0:cut], dests,
                                 T.sem["r%d" % (r - g0)], pick(dests[0], n_row))], local_sem=T.sem.snd)

    def rowbuf(k):
        return T.own if k == r else T["row%d" % (k - g0)]

    def tile(k, s):
        return rowbuf(k)[:, (s + 1) * W:(s + 2) * W]

    def bvec(k, h):
        return rowbuf(k)[:, h * HW:(h + 1) * HW]

    seen = {}

    def need(q, qname, sem, val):
        if (qname, sem) not in seen:
            seen[(qname, sem)] = 1
            q.wait_ge(T.sem[sem], val)

    def need_row(q, qname, k):
        if k == r:
            need(q, qname, "ld", n_ld)
        else:
            need(q, qname, "r%d" % (k - g0), n_row)

    def slot(buf, j, h):
        return buf[:, h * 4 * HW + j * HW: h * 4 * HW + (j + 1) * HW]

    def store(q, sem, val, h, src):
        q.wait_ge(T.sem[sem], val)
        q.dma_start(T.y[:, h * HW:(h + 1) * HW], src).then_inc(T.sem.st, 16)
        n_st[0] += 16

    def idx(k, h):
        return (k - g0) * 2 + h

    if gi == 2:
        def need_own(q, qname, s):
            need(q, qname, "l%d" % cid(s), 16)

        if dests:
            for f, (s0, n) in enumerate(chunks):
                bank = T["ps%d" % (2 + f)]
                need(pe, "pe", "idd", 1)
                need_own(pe, "pe", s0)
                for j in range(n):
                    mm = pe.matmul(bank[:, j * W:(j + 1) * W], tile(r, s0 + j), T.idn[:, :], True, True)
                mm.then_inc(T.sem["tp%d" % f], 1)
                ve.wait_ge(T.sem["tp%d" % f], 1)
                ve.tensor_copy(T.tx[:, (s0 + 1) * W:(s0 + n + 1) * W], bank[:, 0:n * W]).then_inc(T.sem["tc%d" % f], 1)
            for f, (s0, n) in enumerate(chunks):
                lo = (s0 + 1) * W
                hi = (s0 + n + 1) * W
                g.wait_ge(T.sem["tc%d" % f], 1)
                g.remote_dma_fused([xfer(T.tx[:, lo:hi], myrow[:, lo:hi], dests,
                                         T.sem["c%d_%d" % (r - g0, cid(s0))], pick(dests[0], n_row))],
                                   local_sem=T.sem.snd)
            g.wait_ge(T.sem.ld, n_ld)
            g.remote_dma_fused([xfer(T.own[:, 0:W], myrow[:, 0:W], dests,
                                     T.sem["cb%d" % (r - g0)], pick(dests[0], n_row))], local_sem=T.sem.snd)

        on_die = same_die(r, GC)
        n_sya = n_off if r == on_die[0] else n_row
        if r == on_die[0] and len(on_die) > 1:
            g.wait_ge(T.sem.sya, n_off)
            g.remote_dma_fused([xfer(T.ya[:, :], T.ya[:, :], on_die[1:], T.sem.sya, pick(on_die[1], n_row))],
                               local_sem=T.sem.snd)

        def a_t(k, s):
            need(pe, "pe", "c%d_%d" % (k - g0, cid(s)), n_row)
            return T["row%d" % (k - g0)][:, (s + 1) * W:(s + 2) * W]

        def u_ap(k):
            return tile(r, k) if k == r - 1 else T.ub[:, (r - 2 - k) * W:(r - 1 - k) * W]

        def need_u(k):
            if k == r - 1:
                need_own(pe, "pe", k)
            else:
                need(pe, "pe", "uc%d" % (r - 2 - k), 1)

        for kk in lower[1:]:
            j = r - 2 - kk
            ms = [m for m in lower if m > kk]
            for m in ms:
                lt = a_t(m, kk)
                need_u(m)
                mm = pe.matmul(T["ps%d" % (5 + j)][:, 0:W], lt, u_ap(m), m == ms[0], m == ms[-1])
            mm.then_inc(T.sem["up%d" % j], 1)
            ve.wait_ge(T.sem["up%d" % j], 1)
            need_own(ve, "ve", kk)
            ve.tensor_tensor(u_ap(kk), tile(r, kk), T["ps%d" % (5 + j)][:, 0:W],
                             AluOpType.subtract).then_inc(T.sem["uc%d" % j], 1)
        m_bank = (7, 5)
        if lower:
            for blk in (0, 1):
                for s in range(4 * blk, 4 * blk + 4):
                    for k in lower:
                        lt = a_t(k, s)
                        need_u(k)
                        mm = pe.matmul(T["ps%d" % m_bank[blk]][:, (s % 4) * W:(s % 4 + 1) * W], lt, u_ap(k),
                                       k == lower[0], k == lower[-1])
                mm.then_inc(T.sem["mp%d" % blk], 1)
                ve.wait_ge(T.sem["mp%d" % blk], 1)
                need_own(ve, "ve", 4 * blk)
                ve.tensor_tensor(T.mt[:, blk * 512:(blk + 1) * 512], T.own[:, W + blk * 512:W + (blk + 1) * 512],
                                 T["ps%d" % m_bank[blk]][:, 0:512], AluOpType.subtract).then_inc(T.sem["mc%d" % blk], 1)

        def m_ap(s):
            if lower:
                return T.mt[:, s * W:(s + 1) * W]
            need_own(pe, "pe", s)
            return tile(r, s)

        first = {0: True, 1: True}

        def acc(h, lt, rh, stop):
            mm = pe.matmul(T["ps%d" % h][:, 0:HW], lt, rh, first[h], stop)
            first[h] = False
            return mm

        for k in lower:
            need(pe, "pe", "cb%d" % (k - g0), n_row)
            need_u(k)
            for h in (0, 1):
                acc(h, u_ap(k), bvec(k, h), False)
        if lower:
            need(pe, "pe", "mc0", 1)
        need(pe, "pe", "sya", n_sya)
        for h in (0, 1):
            for s in GA:
                acc(h, m_ap(s), slot(T.ya, s - GA[0], h), False)
        if lower:
            need(pe, "pe", "mc1", 1)
        for h in (0, 1):
            need(pe, "pe", "sye%d" % h, n_off)
            acc(h, m_ap(GB[0]), slot(T.yb, 0, h), False)
        for h in (0, 1):
            need(pe, "pe", "syb%d" % h, n_off)
            for s in GB[1:]:
                mm = acc(h, m_ap(s), slot(T.yb, s - GB[0], h), s == GB[-1])
            mm.then_inc(T.sem["p%d" % h], 1)
        need(ve, "ve", "ld", n_ld)
        for h in (0, 1):
            ve.wait_ge(T.sem["p%d" % h], 1)
            ve.tensor_tensor(T.yout[:, h * HW:(h + 1) * HW], bvec(r, h), T["ps%d" % h][:, 0:HW],
                             AluOpType.subtract).then_inc(T.sem["d%d" % h], 1)
            store(queues[h], "d%d" % h, 1, h, T.yout[:, h * HW:(h + 1) * HW])
        if sent[0]:
            g.wait_ge(T.sem.snd, sent[0])
        g.wait_ge(T.sem.st, n_st[0])
        return

    if gi == 1:
        h = b_half(r)
        n_ya = n_off // len(same_die(r, GB))
        free = [j * 2 + (1 - h) for j in range(4)]
        top = GB[-1]

        def need_tile(q, qname, k, s):
            if k == r:
                need(q, qname, "ld", n_ld)
            elif s >= g0:
                need(q, qname, "i%d" % (k - g0), n_row)
            else:
                need(q, qname, "r%d" % (k - g0), n_row)

        tpairs = [(m, k) for m in GB[:-1] for k in GB if k < m]
        tbank = T["ps%d" % free[0]]
        need(pe, "pe", "idd", 1)
        for t, (m, k) in enumerate(tpairs):
            need_tile(pe, "pe", m, k)
            mm = pe.matmul(tbank[:, t * W:(t + 1) * W], tile(m, k), T.idn[:, :], True, True)
        mm.then_inc(T.sem.tp0, 1)
        ve.wait_ge(T.sem.tp0, 1)
        ve.tensor_copy(T.bt[:, 0:len(tpairs) * W], tbank[:, 0:len(tpairs) * W]).then_inc(T.sem.tc0, 1)

        def b_t(m, k):
            t = tpairs.index((m, k))
            return T.bt[:, t * W:(t + 1) * W]

        comp = [(kr, k) for kr in GB for k in [m for m in GB if m < kr - 1][::-1]]

        def u_of(kr, k):
            if k == kr - 1:
                return tile(kr, k)
            i = comp.index((kr, k))
            return T.ub[:, i * W:(i + 1) * W]

        def need_uf(kr, k):
            if k == kr - 1:
                need_tile(pe, "pe", kr, k)
            else:
                need(pe, "pe", "uc%d" % comp.index((kr, k)), 1)

        need(pe, "pe", "tc0", 1)
        for i, (kr, k) in enumerate(comp):
            bank = T["ps%d" % free[1 + i]]
            ms = [m for m in GB if k < m < kr][::-1]
            for m in ms:
                need_uf(kr, m)
                mm = pe.matmul(bank[:, 0:W], b_t(m, k), u_of(kr, m), m == ms[0], m == ms[-1])
            mm.then_inc(T.sem["up%d" % i], 1)
            ve.wait_ge(T.sem["up%d" % i], 1)
            need_tile(ve, "ve", kr, k)
            ve.tensor_tensor(u_of(kr, k), tile(kr, k), bank[:, 0:W], AluOpType.subtract).then_inc(T.sem["uc%d" % i], 1)

        def z_ap(m):
            return slot(T.yb, 0, h) if m == g0 else T.zb[:, (m - g0 - 1) * HW:(m - g0) * HW]

        def z_sem(m):
            return "d%d" % idx(g0, h) if m == g0 else "z%d" % (m - g0 - 1)

        for k in GB:
            need_tile(pe, "pe", k, GA[0])
        need(pe, "pe", "sya", n_ya)
        for k in GB:
            for s in GA[:EARLY]:
                pe.matmul(T["ps%d" % idx(k, h)][:, 0:HW], tile(k, s), slot(T.ya, s - GA[0], h), s == GA[0], False)
        need(pe, "pe", "sya2", n_ya)
        for k in GB:
            for s in GA[EARLY:]:
                mm = pe.matmul(T["ps%d" % idx(k, h)][:, 0:HW], tile(k, s), slot(T.ya, s - GA[0], h),
                               False, s == GA[-1] and k != top)
            if k != top:
                mm.then_inc(T.sem["p%d" % idx(k, h)], 1)
        for k in GB[:-1]:
            need_tile(ve, "ve", k, GA[0])
            ve.wait_ge(T.sem["p%d" % idx(k, h)], 1)
            ve.tensor_tensor(z_ap(k), bvec(k, h), T["ps%d" % idx(k, h)][:, 0:HW],
                             AluOpType.subtract).then_inc(T.sem[z_sem(k)], 1)

        def bank2(k):
            return T["ps%d" % idx(k, h)] if k == top else T["ps%d" % free[k - g0 - 1]]

        for i in range(len(comp)):
            need(pe, "pe", "uc%d" % i, 1)
        for m in GB[:-1]:
            need(pe, "pe", z_sem(m), 1)
            for k in GB:
                if k <= m:
                    continue
                need_uf(k, m)
                mm = pe.matmul(bank2(k)[:, 0:HW], u_of(k, m), z_ap(m), m == g0 and k != top, m == k - 1)
                if m == k - 1:
                    mm.then_inc(T.sem["q%d" % (k - g0 - 1)], 1)
        for k in GB[1:]:
            ve.wait_ge(T.sem["q%d" % (k - g0 - 1)], 1)
            if k == top:
                need_tile(ve, "ve", k, GA[0])
                src = bvec(k, h)
            else:
                need(ve, "ve", z_sem(k), 1)
                src = z_ap(k)
            ve.tensor_tensor(slot(T.yb, k - g0, h), src, bank2(k)[:, 0:HW],
                             AluOpType.subtract).then_inc(T.sem["d%d" % idx(k, h)], 1)

        mine_c = same_die(r, GC)
        g.wait_ge(T.sem["d%d" % idx(g0, h)], 1)
        g.remote_dma_fused([xfer(slot(T.yb, 0, h), slot(T.yb, 0, h), mine_c, T.sem["sye%d" % h],
                                 pick(mine_c[0], n_off))], local_sem=T.sem.snd)
        for k in GB[1:]:
            g.wait_ge(T.sem["d%d" % idx(k, h)], 1)
        g.remote_dma_fused([xfer(T.yb[:, h * 4 * HW + HW:(h + 1) * 4 * HW], T.yb[:, h * 4 * HW + HW:(h + 1) * 4 * HW],
                                 mine_c, T.sem["syb%d" % h], pick(mine_c[0], n_off))], local_sem=T.sem.snd)
        partner = [q for q in same_die(r, GB) if q != r][0]
        g.remote_dma_fused([xfer(slot(T.yb, partner - g0, h), T.xch[:, 0:HW], [partner], T.sem.sx,
                                 pick(partner, n_off, home))], local_sem=T.sem.snd)
        store(g.sync, "d%d" % idx(r, h), 1, h, slot(T.yb, r - g0, h))
        store(g.scalar, "sx", n_off, 1 - h, T.xch[:, 0:HW])
        g.wait_ge(T.sem.snd, sent[0])
        g.wait_ge(T.sem.st, n_st[0])
        return

    rows = list(GA) if r in solvers else []
    halves = [0, 1]
    yloc = T.ya

    def terms(k, h):
        out = []
        for s in range(k):
            if s == g0:
                out.append((tile(k, s), bvec(s, h), None))
            else:
                out.append((tile(k, s), slot(yloc, s - g0, h), "d%d" % idx(s, h)))
        return out

    for k in rows:
        tl = {h: terms(k, h) for h in halves}
        nt = len(tl[halves[0]])
        if nt == 0:
            for h in halves:
                need_row(ve, "ve", k)
                ve.tensor_copy(slot(yloc, k - g0, h), bvec(k, h)).then_inc(T.sem["d%d" % idx(k, h)], 1)
            continue
        for h, n in [(h, n) for n in range(nt) for h in halves]:
            lt, rh, sem = tl[h][n]
            need_row(pe, "pe", k)
            if sem is None:
                need_row(pe, "pe", g0)
            else:
                need(pe, "pe", sem, 1)
            mm = pe.matmul(T["ps%d" % idx(k, h)][:, 0:HW], lt, rh, n == 0, n == nt - 1)
            if n == nt - 1:
                mm.then_inc(T.sem["p%d" % idx(k, h)], 1)
        for h in halves:
            need_row(ve, "ve", k)
            ve.wait_ge(T.sem["p%d" % idx(k, h)], 1)
            ve.tensor_tensor(slot(yloc, k - g0, h), bvec(k, h), T["ps%d" % idx(k, h)][:, 0:HW],
                             AluOpType.subtract).then_inc(T.sem["d%d" % idx(k, h)], 1)

    if r in solvers:
        mine_b = same_die(r, GB)
        per = n_off // len(mine_b)

        def piece(hh, j0, j1):
            return T.ya[:, hh * 4 * HW + j0 * HW: hh * 4 * HW + j1 * HW]

        for (j0, j1, sem) in ((0, EARLY, T.sem.sya), (EARLY, len(rows), T.sem.sya2)):
            for k in rows[j0:j1]:
                for h in halves:
                    g.wait_ge(T.sem["d%d" % idx(k, h)], 1)
            g.remote_dma_fused([xfer(piece(b_half(q), j0, j1), piece(b_half(q), j0, j1),
                                     [q], sem, pick(q, per, j * per)) for j, q in enumerate(mine_b)],
                               local_sem=T.sem.snd)
        first_c = same_die(r, GC)[0]
        g.remote_dma_fused([xfer(T.ya[:, :], T.ya[:, :], [first_c], T.sem.sya, pick(first_c, n_off))],
                           local_sem=T.sem.snd)
        for q in GA:
            if q != g0 and q not in solvers and same_die(q, solvers)[0] == r:
                per = n_off // 2
                g.remote_dma_fused([xfer(slot(T.ya, q - g0, h), T.xch[:, h * HW:(h + 1) * HW], [q], T.sem.sx,
                                         pick(q, per, home + h * per)) for h in (0, 1)], local_sem=T.sem.snd)
        for h in halves:
            store(queues[h], "d%d" % idx(r, h), 1, h, slot(T.ya, r - g0, h))
    elif r == g0:
        g.scalar.wait_ge(T.sem.ld, n_ld)
        g.scalar.dma_start(T.y[:, :], T.own[:, 0:W]).then_inc(T.sem.st, 16)
        n_st[0] += 16
    else:
        g.sync.wait_ge(T.sem.sx, n_off)
        g.sync.dma_start(T.y[:, :], T.xch[:, :]).then_inc(T.sem.st, 16)
        n_st[0] += 16

    if sent[0]:
        g.wait_ge(T.sem.snd, sent[0])
    g.wait_ge(T.sem.st, n_st[0])
